import numpy as np
import ml_dtypes


def mxq(x, axis, fmt="e4m3"):
    dtype, down = {"e4m3": (ml_dtypes.float8_e4m3fn, 7), "e5m2": (ml_dtypes.float8_e5m2, 14)}[fmt]
    v = np.moveaxis(np.asarray(x, np.float32).astype(ml_dtypes.bfloat16).astype(np.float64), axis, -1)
    blocks = v.reshape(v.shape[:-1] + (-1, 32))
    amax = np.abs(blocks).max(-1, keepdims=True)
    byte = np.maximum(np.where(amax > 0, np.frexp(amax)[1] - 1 + 127, 0) - down, 1)
    scale = np.exp2(byte - 127.0)
    codes = (blocks / scale).astype(np.float32).astype(dtype).astype(np.float64)
    return np.moveaxis((codes * scale).reshape(v.shape), -1, axis)


WIDE = False


def mx_kscale(k):
    if not WIDE:
        return np.ones(k)
    levels = np.array([10, -10, 5, -5, 0])
    if k % 512:
        return np.exp2(np.random.permutation(np.resize(levels, k // 32))).repeat(32)
    a = np.empty((k // 512, 16))
    for p in range(k // 512):
        a[p, :8] = np.random.permutation(np.resize(levels, 8))
        for g in range(8):
            far = levels[np.abs(levels - a[p, g]) >= 10]
            a[p, g + 8] = far[np.random.randint(len(far))]
    return np.exp2(a.ravel()).repeat(32)


def f64(x):
    return np.asarray(x).astype(np.float64)


def striped(idx):
    return np.tile(np.asarray(idx).reshape(-1, 16).T, (8, 1)).astype(np.uint16)


def unstriped(offs):
    return offs[:16].T.reshape(-1).astype(np.int64)


E2M1 = np.array([0.0, 0.5, 1.0, 1.5, 2.0, 3.0, 4.0, 6.0, -0.0, -0.5, -1.0, -1.5, -2.0, -3.0, -4.0, -6.0])


def pack_weight(w, fmt):
    k, n = w.shape
    w = f64(np.asarray(w, np.float32).astype(ml_dtypes.bfloat16)).reshape(k // 32, 32, n)
    amax = np.abs(w).max(1)
    if fmt == "e4m3":
        byte = np.frexp(amax)[1] - 1 + 127 - 7
    else:
        mant, ex = np.frexp(amax / 6.0)
        byte = np.where(mant > 0.5, ex, ex - 1) + 127
    byte = np.clip(np.where(amax > 0, byte, 1), 1, 254)
    scaled = (w * np.exp2(127.0 - byte)[:, None, :]).reshape(k, n).astype(np.float32)
    by_word = np.ascontiguousarray(scaled.reshape(k // 512, 128, 4, n).transpose(0, 1, 3, 2))
    if fmt == "e4m3":
        words = by_word.astype(ml_dtypes.float8_e4m3fn).view(np.uint8)
    else:
        c = by_word.astype(ml_dtypes.float4_e2m1fn).view(np.uint8) & 0xF
        words = (c[..., 0::2] | (c[..., 1::2] << 4)).reshape(k // 512, 128, 2 * n)
    return np.ascontiguousarray(words), np.ascontiguousarray(byte.astype(np.uint8).reshape(k // 512, 16, n))


def unpack_weight(words, scales, fmt):
    g, _, n = scales.shape
    words = np.ascontiguousarray(words).reshape(g, 128, n, -1)
    if fmt == "e4m3":
        vals = words.view(ml_dtypes.float8_e4m3fn).astype(np.float64)
    else:
        nib = np.empty((g, 128, n, 4), np.uint8)
        nib[..., 0::2] = words & 0xF
        nib[..., 1::2] = words >> 4
        vals = E2M1[nib]
    vals = vals * np.repeat(np.exp2(scales.astype(np.float64) - 127.0), 8, axis=1)[..., None]
    return vals.transpose(0, 1, 3, 2).reshape(g * 512, n)


def bf(x):
    return np.asarray(x, np.float32).astype(ml_dtypes.bfloat16)


def planes(Y):
    r, m = Y.shape
    b = f64(bf(Y)).reshape(r // 32, 32, m)
    amax = np.abs(b).max(1)
    byte = np.clip(np.where(amax > 0, np.frexp(amax)[1] - 1 + 127 - 7, 1), 1, 254)
    codes = (b * np.exp2(127.0 - byte)[:, None, :]).reshape(r, m).astype(np.float32).astype(ml_dtypes.float8_e4m3fn).view(np.uint8)
    words = codes.reshape(r // 512, 128, 4, m).transpose(0, 1, 3, 2)
    return np.ascontiguousarray(words), np.ascontiguousarray(byte.astype(np.uint8).reshape(r // 512, 16, m))


K, L, T, J, N = 1024, 512, 1024, 512, 512


def setup_inputs():
    n = np.random.standard_normal
    idx = np.random.permutation(T)[:J]
    fk = mx_kscale(K)
    fl = mx_kscale(L)
    xtp = pack_weight(n((K, T)) / fk[:, None], "e2m1")
    xep = pack_weight(n((L, J)) / fl[:, None], "e4m3")
    wep = pack_weight(n((L, N)) * 1 / np.sqrt(L) * fl[:, None], "e2m1")
    return {
        "xt_words": xtp[0],
        "xt_scales": xtp[1],
        "ws": (n((K, N)) * 1 / np.sqrt(K) * fk[:, None]).astype(np.float32),
        "xe_words": xep[0],
        "xe_scales": xep[1],
        "we_words": wep[0],
        "we_scales": wep[1],
        "bd": (np.random.uniform(0.3, 1.0, (N, 1))).astype(np.float32),
        "rw": (np.random.uniform(0.5, 2.0, (1, J))).astype(np.float32),
        "offs": striped(idx),
    }


def reference(xt_words, xt_scales, ws, xe_words, xe_scales, we_words, we_scales, bd, rw, offs):
    idx = unstriped(offs)
    xtu = unpack_weight(xt_words, xt_scales, "e2m1")
    xeu = unpack_weight(xe_words, xe_scales, "e4m3")
    weu = unpack_weight(we_words, we_scales, "e2m1")
    wsq = mxq(f64(ws), 0, "e4m3")
    u = wsq.T @ xtu
    p = weu.T @ xeu
    h1 = np.minimum(p, u[:, idx] + f64(bd))
    y = np.maximum(h1, u[:, idx] - f64(bd)) * f64(rw)
    words, scales = planes(y)
    return y, words, scales

@@ -1,0 +1,259 @@
+from contextlib import ExitStack
+
+import concourse.mybir as mybir
+from concourse.masks import make_identity
+
+K, L, T, J, N = 1024, 512, 1024, 512, 512
+FLOPS = 2 * K * N * T + 2 * L * N * J
+
+F32 = mybir.dt.float32
+BF16 = mybir.dt.bfloat16
+I32 = mybir.dt.int32
+U32 = mybir.dt.uint32
+U16 = mybir.dt.uint16
+U8 = mybir.dt.uint8
+FP8X4 = mybir.dt.float8_e4m3fn_x4
+FP4X4 = mybir.dt.float4_e2m1fn_x4
+ALU = mybir.AluOpType
+
+P = 128
+PACK = 4
+K_PASS = P * PACK
+BANK = 512
+LIST_GROUP = 16
+J_MAIN = 384
+CAST_VECTOR_EIGHTHS = 5
+
+
+def tile_moe_expert_held_near_shared_pl_kernel(
+    tc, xt_words, xt_scales, ws, xe_words, xe_scales, we_words, we_scales, bd, rw, offs, out_0, out_1, out_2
+):
+    nc = tc.nc
+    passes = K // K_PASS
+    halves = T // BANK
+
+    with ExitStack() as ctx:
+        sb = ctx.enter_context(tc.tile_pool(name="sb", bufs=1))
+        psum = ctx.enter_context(tc.psum_pool(name="psum", bufs=1))
+
+        def load_scale_rows(queue, plane, rows):
+            for q in range(4):
+                queue.dma_start(
+                    out=plane[32 * q : 32 * q + 4].bitcast(I32),
+                    in_=rows[:, 4 * q : 4 * q + 4, :].rearrange("z r c -> r z c").bitcast(I32),
+                )
+
+        xt_plane = sb.tile([P, passes, T], U8, align_bytes=64)
+        xe_plane = sb.tile([P, 1, J], U8, align_bytes=64)
+        we_plane_raw = sb.tile([P, 1, N], U8, align_bytes=64)
+        nc.vector.memset(we_plane_raw[:].bitcast(I32), 0)
+
+        band = sb.tile([P, PACK], F32)
+        rw_cols = sb.tile([P, PACK], F32)
+        identity = sb.tile([P, P], F32)
+        make_identity(nc, identity[:])
+
+        ws_pieces = [(0, 0, N), (1, 0, N // 2), (1, N // 2, N)]
+        ws_raw = [sb.tile([P, PACK, c1 - c0], F32, name=f"ws_raw{i}") for i, (g, c0, c1) in enumerate(ws_pieces)]
+        xt_codes = sb.tile([P, passes, 2 * T], U8, align_bytes=64)
+
+        def load_ws(i):
+            g, c0, c1 = ws_pieces[i]
+            rows = ws[g * K_PASS : (g + 1) * K_PASS, c0:c1]
+            nc.sync.dma_start(out=ws_raw[i][:], in_=rows.rearrange("(p j) n -> p j n", j=PACK))
+
+        offsets = sb.tile([P, J // LIST_GROUP], U16)
+        nc.sync.dma_start(offsets[:], offs)
+        load_scale_rows(nc.scalar, xt_plane, xt_scales)
+        load_ws(0)
+        nc.sync.dma_start(out=xt_codes[:].bitcast(I32), in_=xt_words.rearrange("z p c -> p z c").bitcast(I32))
+        nc.sync.dma_start(out=band[:], in_=bd.rearrange("(p t) o -> p (t o)", t=PACK))
+        load_ws(1)
+        nc.scalar.dma_start(out=rw_cols[:], in_=rw.rearrange("o (p c) -> (o p) c", c=PACK))
+        load_ws(2)
+        we_raw = sb.tile([P, 2 * N], U8, align_bytes=64)
+        nc.sync.dma_start(out=we_raw[:].bitcast(I32), in_=we_words[0].bitcast(I32))
+        load_scale_rows(nc.sync, we_plane_raw, we_scales)
+        xe_codes = sb.tile([P, PACK * J], U8, align_bytes=64)
+        nc.sync.dma_start(out=xe_codes[:].bitcast(I32), in_=xe_words[0].rearrange("p c r -> p (c r)").bitcast(I32))
+        load_scale_rows(nc.gpsimd, xe_plane, xe_scales)
+
+        rw_bank = psum.tile([P, PACK, P], F32, tag="p3")
+        for c in range(PACK):
+            nc.tensor.transpose(rw_bank[:, c, :], rw_cols[:, c : c + 1].to_broadcast([P, P]), identity[:])
+        rw_rows = sb.tile([P, J], F32)
+        nc.scalar.copy(out=rw_rows[:].rearrange("x (p c) -> x p c", c=PACK), in_=rw_bank[:].rearrange("x c p -> x p c"))
+
+        ws_bf = [sb.tile([P, PACK * N], BF16, name=f"ws_bf{g}", align_bytes=64) for g in range(passes)]
+        ws_codes = [sb.tile([P, N], U32, name=f"ws_codes{g}", align_bytes=64) for g in range(passes)]
+        ws_plane = [sb.tile([P, N], U8, name=f"ws_plane{g}", align_bytes=64) for g in range(passes)]
+
+        def round_ws(i):
+            g, c0, c1 = ws_pieces[i]
+            m0, count = c0 // PACK, (c1 - c0) // PACK
+            cut = count * CAST_VECTOR_EIGHTHS // 8
+            src = ws_raw[i][:].rearrange("p j (m t) -> p m j t", t=PACK)
+            dst = ws_bf[g][:].rearrange("p (t m j) -> p m j t", t=PACK, j=PACK)
+            nc.vector.tensor_copy(out=dst[:, m0 : m0 + cut], in_=src[:, :cut])
+            nc.scalar.copy(out=dst[:, m0 + cut : m0 + count], in_=src[:, cut:])
+
+        def quantise_ws(g, t0, t1):
+            nc.vector.quantize_mx(
+                out=ws_codes[g][:, t0 * P : t1 * P].bitcast(FP8X4),
+                scales=ws_plane[g][:, t0 * P : t1 * P],
+                in_=ws_bf[g][:, t0 * K_PASS : t1 * K_PASS],
+            )
+
+        round_ws(0)
+        quantise_ws(0, 0, 4)
+        round_ws(1)
+        round_ws(2)
+        quantise_ws(1, 0, 1)
+        quantise_ws(1, 1, 2)
+        quantise_ws(1, 2, 4)
+
+        u_banks = {}
+
+        def shared_pass(t, h, g):
+            if g == 0:
+                u_banks[t, h] = psum.tile([P, BANK], F32, name=f"u_bank{t}{h}", tag=f"u{(halves * t + h) % 4}")
+            nc.tensor.matmul_mx(
+                out=u_banks[t, h][:],
+                lhsT=ws_codes[g][:, t * P : (t + 1) * P].bitcast(FP8X4),
+                lhsT_scale=ws_plane[g][:, t * P : (t + 1) * P],
+                rhs=xt_codes[:, g, 2 * h * BANK : 2 * (h + 1) * BANK].bitcast(FP4X4),
+                rhs_scale=xt_plane[:, g, h * BANK : (h + 1) * BANK],
+                start=(g == 0),
+                stop=(g == passes - 1),
+            )
+
+        u_rows = [sb.tile([P, T], F32, name=f"u_rows{t}") for t in range(PACK)]
+
+        def empty_u(t, h):
+            dst = u_rows[t][:, h * BANK : (h + 1) * BANK]
+            if (t, h) == (0, 1):
+                nc.vector.tensor_copy(out=dst, in_=u_banks[t, h][:])
+            else:
+                nc.scalar.copy(out=dst, in_=u_banks[t, h][:])
+
+        for g in range(passes):
+            for t in range(2):
+                for h in range(halves):
+                    shared_pass(t, h, g)
+
+        we_codes = sb.tile([P, 2 * N], U8, align_bytes=64)
+        we_plane = sb.tile([P, N], U8, align_bytes=64)
+        nc.vector.tensor_copy(
+            out=we_codes[:].bitcast(U16).rearrange("p (t m) -> p t m", t=PACK),
+            in_=we_raw[:].bitcast(U16).rearrange("p (m t) -> p t m", t=PACK),
+        )
+        nc.vector.tensor_copy(
+            out=we_plane[:].rearrange("p (t m) -> p t m", t=PACK),
+            in_=we_plane_raw[:, 0, :].rearrange("p (m t) -> p t m", t=PACK),
+        )
+        for t in range(2):
+            for h in range(halves):
+                empty_u(t, h)
+
+        p_banks = []
+        for t in range(PACK):
+            p_bank = psum.tile([P, J], F32, name=f"p_bank{t}", tag=f"p{t}")
+            nc.tensor.matmul_mx(
+                out=p_bank[:],
+                lhsT=we_codes[:, 2 * t * P : 2 * (t + 1) * P].bitcast(FP4X4),
+                lhsT_scale=we_plane[:, t * P : (t + 1) * P],
+                rhs=xe_codes[:].bitcast(FP8X4),
+                rhs_scale=xe_plane[:, 0, :],
+                start=True,
+                stop=True,
+            )
+            p_banks.append(p_bank)
+        for t in range(2, PACK):
+            for h in range(halves):
+                for g in range(passes):
+                    shared_pass(t, h, g)
+                empty_u(t, h)
+
+        out_rows = out_0.rearrange("(p t) j -> p t j", t=PACK)
+        out_words = out_1[0].rearrange("p c r -> p (c r)").bitcast(I32)
+        y_codes = sb.tile([P, J], U32, align_bytes=64)
+        y_plane = sb.tile([P, J], U8, align_bytes=64)
+        y_bf = sb.tile([P, J, PACK], BF16, align_bytes=64)
+
+        stretches = [(0, J_MAIN), (J_MAIN, J)]
+        near = [[sb.tile([P, j1 - j0], F32, name=f"near{s}{t}") for t in range(PACK)] for s, (j0, j1) in enumerate(stretches)]
+        capped = [[sb.tile([P, j1 - j0], F32, name=f"capped{s}{t}") for t in range(PACK)] for s, (j0, j1) in enumerate(stretches)]
+        held = [sb.tile([P, PACK, j1 - j0], F32, name=f"held{s}") for s, (j0, j1) in enumerate(stretches)]
+        y = [sb.tile([P, PACK, j1 - j0], F32, name=f"y{s}") for s, (j0, j1) in enumerate(stretches)]
+
+        def look_up(s, t):
+            j0, j1 = stretches[s]
+            nc.vector.tensor_copy(near[s][t][:], u_rows[t][:].indirect(offsets[:, j0 // LIST_GROUP : j1 // LIST_GROUP]))
+
+        def cap(s, t):
+            j0, j1 = stretches[s]
+            nc.vector.scalar_tensor_tensor(
+                out=capped[s][t][:], in0=near[s][t][:], scalar=band[:, t : t + 1], in1=p_banks[t][:, j0:j1],
+                op0=ALU.add, op1=ALU.min,
+            )
+
+        def floor_at(s, t):
+            nc.vector.scalar_tensor_tensor(
+                out=held[s][:, t, :], in0=near[s][t][:], scalar=band[:, t : t + 1], in1=capped[s][t][:],
+                op0=ALU.subtract, op1=ALU.max,
+            )
+
+        def weigh(t):
+            nc.vector.tensor_tensor(out=y[0][:, t, :], in0=held[0][:, t, :], in1=rw_rows[:, :J_MAIN], op=ALU.mult)
+            nc.sync.dma_start(out=out_rows[:, t, :J_MAIN], in_=y[0][:, t, :])
+
+        def round_y(copy, s, j0, j1):
+            base = stretches[s][0]
+            copy(
+                out=y_bf[:, j0:j1, :].rearrange("p (c i) t -> p c t i", i=4),
+                in_=y[s][:, :, j0 - base : j1 - base].rearrange("p t (c i) -> p c t i", i=4),
+            )
+
+        def quantise_y(j0, j1):
+            nc.vector.quantize_mx(
+                out=y_codes[:, j0:j1].bitcast(FP8X4),
+                scales=y_plane[:, j0:j1],
+                in_=y_bf[:, j0:j1, :].rearrange("p j t -> p (j t)"),
+            )
+
+        look_up(0, 0)
+        cap(0, 0)
+        for t in range(1, PACK):
+            look_up(0, t)
+            floor_at(0, t - 1)
+            cap(0, t)
+            weigh(t - 1)
+        look_up(1, 0)
+        floor_at(0, PACK - 1)
+        look_up(1, 1)
+        weigh(PACK - 1)
+        round_y(nc.scalar.copy, 0, 0, 256)
+        round_y(nc.scalar.copy, 0, 256, J_MAIN)
+        look_up(1, 2)
+        look_up(1, 3)
+        for t in range(PACK):
+            cap(1, t)
+        for t in range(PACK):
+            floor_at(1, t)
+        quantise_y(0, 256)
+        nc.vector.tensor_tensor(
+            out=y[1][:], in0=held[1][:],
+            in1=rw_rows[:, J_MAIN:].unsqueeze(1).to_broadcast([P, PACK, J - J_MAIN]), op=ALU.mult,
+        )
+        nc.sync.dma_start(out=out_rows[:, :, J_MAIN:], in_=y[1][:])
+        quantise_y(256, J_MAIN)
+        nc.sync.dma_start(out=out_words[:, :J_MAIN], in_=y_codes[:, :J_MAIN].bitcast(I32))
+        round_y(nc.vector.tensor_copy, 1, J_MAIN, J)
+        quantise_y(J_MAIN, J)
+        nc.sync.dma_start(out=out_words[:, J_MAIN:], in_=y_codes[:, J_MAIN:].bitcast(I32))
+        for q in range(4):
+            queue = nc.scalar if q % 2 == 0 else nc.sync
+            queue.dma_start(
+                out=out_2[0, 4 * q : 4 * q + 4, :].bitcast(I32),
+                in_=y_plane[32 * q : 32 * q + 4, :].bitcast(I32),
+            )

@@ -1,7 +1,6 @@
 from contextlib import ExitStack
 
 import concourse.mybir as mybir
-from concourse.masks import make_identity
 
 K, L, T, J, N = 1024, 512, 1024, 512, 512
 FLOPS = 2 * K * N * T + 2 * L * N * J
@@ -15,6 +14,7 @@ U8 = mybir.dt.uint8
 FP8X4 = mybir.dt.float8_e4m3fn_x4
 FP4X4 = mybir.dt.float4_e2m1fn_x4
 ALU = mybir.AluOpType
+ACT = mybir.ActivationFunctionType
 
 P = 128
 PACK = 4
@@ -51,38 +51,47 @@ def tile_moe_expert_held_near_shared_pl_kernel(
         band = sb.tile([P, PACK], F32)
         rw_cols = sb.tile([P, PACK], F32)
         identity = sb.tile([P, P], F32)
-        make_identity(nc, identity[:])
+        column_less_row = sb.tile([P, P], I32)
+        nc.gpsimd.iota(column_less_row[:], pattern=[[1, P]], base=0, channel_multiplier=-1)
+        nc.vector.tensor_scalar(out=identity[:], in0=column_less_row[:], scalar1=0.0, scalar2=None, op0=ALU.is_equal)
 
-        ws_pieces = [(0, 0, N), (1, 0, N // 2), (1, N // 2, N)]
-        ws_raw = [sb.tile([P, PACK, c1 - c0], F32, name=f"ws_raw{i}") for i, (g, c0, c1) in enumerate(ws_pieces)]
-        xt_codes = sb.tile([P, passes, 2 * T], U8, align_bytes=64)
+        ws_pieces = [(0, 0, N // 2), (0, N // 2, N), (1, 0, N // 2), (1, N // 2, N)]
+        ws_raw = [sb.tile([P, PACK, c1 - c0], F32, name=f"ws_raw{i}", tag=f"ws_raw{i}", align_bytes=64) for i, (g, c0, c1) in enumerate(ws_pieces)]
+        xt_codes = [sb.tile([P, 2 * T], U8, name=f"xt_codes{g}", align_bytes=64) for g in range(passes)]
 
         def load_ws(i):
             g, c0, c1 = ws_pieces[i]
             rows = ws[g * K_PASS : (g + 1) * K_PASS, c0:c1]
             nc.sync.dma_start(out=ws_raw[i][:], in_=rows.rearrange("(p j) n -> p j n", j=PACK))
 
-        offsets = sb.tile([P, J // LIST_GROUP], U16)
-        nc.sync.dma_start(offsets[:], offs)
-        load_scale_rows(nc.scalar, xt_plane, xt_scales)
+        nc.gpsimd.dma_start(out=rw_cols[:], in_=rw.rearrange("o (p c) -> (o p) c", c=PACK))
+        load_scale_rows(nc.gpsimd, we_plane_raw, we_scales)
         load_ws(0)
-        nc.sync.dma_start(out=xt_codes[:].bitcast(I32), in_=xt_words.rearrange("z p c -> p z c").bitcast(I32))
-        nc.sync.dma_start(out=band[:], in_=bd.rearrange("(p t) o -> p (t o)", t=PACK))
         load_ws(1)
-        nc.scalar.dma_start(out=rw_cols[:], in_=rw.rearrange("o (p c) -> (o p) c", c=PACK))
-        load_ws(2)
+        load_scale_rows(nc.sync, xt_plane, xt_scales)
+        nc.sync.dma_start(out=xt_codes[0][:].bitcast(I32), in_=xt_words[0].bitcast(I32))
         we_raw = sb.tile([P, 2 * N], U8, align_bytes=64)
         nc.sync.dma_start(out=we_raw[:].bitcast(I32), in_=we_words[0].bitcast(I32))
-        load_scale_rows(nc.sync, we_plane_raw, we_scales)
+        load_ws(2)
+        load_ws(3)
+        nc.sync.dma_start(out=xt_codes[1][:].bitcast(I32), in_=xt_words[1].bitcast(I32))
+        nc.sync.dma_start(out=band[:], in_=bd.rearrange("(p t) o -> p (t o)", t=PACK))
+        offsets = sb.tile([P, J // LIST_GROUP], U16)
+        nc.sync.dma_start(offsets[:], offs)
         xe_codes = sb.tile([P, PACK * J], U8, align_bytes=64)
         nc.sync.dma_start(out=xe_codes[:].bitcast(I32), in_=xe_words[0].rearrange("p c r -> p (c r)").bitcast(I32))
-        load_scale_rows(nc.gpsimd, xe_plane, xe_scales)
+        load_scale_rows(nc.sync, xe_plane, xe_scales)
 
         rw_bank = psum.tile([P, PACK, P], F32, tag="p3")
         for c in range(PACK):
             nc.tensor.transpose(rw_bank[:, c, :], rw_cols[:, c : c + 1].to_broadcast([P, P]), identity[:])
         rw_rows = sb.tile([P, J], F32)
         nc.scalar.copy(out=rw_rows[:].rearrange("x (p c) -> x p c", c=PACK), in_=rw_bank[:].rearrange("x c p -> x p c"))
+
+        minus_band = sb.tile([P, PACK], F32)
+        twice_band = sb.tile([P, PACK], F32)
+        nc.vector.tensor_scalar(out=minus_band[:], in0=band[:], scalar1=-1.0, scalar2=None, op0=ALU.mult)
+        nc.vector.tensor_scalar(out=twice_band[:], in0=band[:], scalar1=2.0, scalar2=None, op0=ALU.mult)
 
         ws_bf = [sb.tile([P, PACK * N], BF16, name=f"ws_bf{g}", align_bytes=64) for g in range(passes)]
         ws_codes = [sb.tile([P, N], U32, name=f"ws_codes{g}", align_bytes=64) for g in range(passes)]
@@ -104,13 +113,12 @@ def tile_moe_expert_held_near_shared_pl_kernel(
                 in_=ws_bf[g][:, t0 * K_PASS : t1 * K_PASS],
             )
 
-        round_ws(0)
-        quantise_ws(0, 0, 4)
-        round_ws(1)
-        round_ws(2)
-        quantise_ws(1, 0, 1)
-        quantise_ws(1, 1, 2)
-        quantise_ws(1, 2, 4)
+        for g in range(passes):
+            round_ws(2 * g)
+            round_ws(2 * g + 1)
+            quantise_ws(g, 0, 1)
+            quantise_ws(g, 1, 2)
+            quantise_ws(g, 2, 4)
 
         u_banks = {}
 
@@ -121,7 +129,7 @@ def tile_moe_expert_held_near_shared_pl_kernel(
                 out=u_banks[t, h][:],
                 lhsT=ws_codes[g][:, t * P : (t + 1) * P].bitcast(FP8X4),
                 lhsT_scale=ws_plane[g][:, t * P : (t + 1) * P],
-                rhs=xt_codes[:, g, 2 * h * BANK : 2 * (h + 1) * BANK].bitcast(FP4X4),
+                rhs=xt_codes[g][:, 2 * h * BANK : 2 * (h + 1) * BANK].bitcast(FP4X4),
                 rhs_scale=xt_plane[:, g, h * BANK : (h + 1) * BANK],
                 start=(g == 0),
                 stop=(g == passes - 1),
@@ -132,9 +140,11 @@ def tile_moe_expert_held_near_shared_pl_kernel(
         def empty_u(t, h):
             dst = u_rows[t][:, h * BANK : (h + 1) * BANK]
             if (t, h) == (0, 1):
-                nc.vector.tensor_copy(out=dst, in_=u_banks[t, h][:])
+                nc.vector.tensor_scalar(
+                    out=dst, in0=u_banks[t, h][:], scalar1=minus_band[:, t : t + 1], scalar2=None, op0=ALU.add
+                )
             else:
-                nc.scalar.copy(out=dst, in_=u_banks[t, h][:])
+                nc.scalar.activation(out=dst, in_=u_banks[t, h][:], func=ACT.Identity, bias=minus_band[:, t : t + 1])
 
         for g in range(passes):
             for t in range(2):
@@ -142,7 +152,7 @@ def tile_moe_expert_held_near_shared_pl_kernel(
                     shared_pass(t, h, g)
 
         we_codes = sb.tile([P, 2 * N], U8, align_bytes=64)
-        we_plane = sb.tile([P, N], U8, align_bytes=64)
+        we_plane = sb.tile([P, N], U8, tag="ws_raw1", align_bytes=64)
         nc.vector.tensor_copy(
             out=we_codes[:].bitcast(U16).rearrange("p (t m) -> p t m", t=PACK),
             in_=we_raw[:].bitcast(U16).rearrange("p (m t) -> p t m", t=PACK),
@@ -193,15 +203,12 @@ def tile_moe_expert_held_near_shared_pl_kernel(
         def cap(s, t):
             j0, j1 = stretches[s]
             nc.vector.scalar_tensor_tensor(
-                out=capped[s][t][:], in0=near[s][t][:], scalar=band[:, t : t + 1], in1=p_banks[t][:, j0:j1],
+                out=capped[s][t][:], in0=near[s][t][:], scalar=twice_band[:, t : t + 1], in1=p_banks[t][:, j0:j1],
                 op0=ALU.add, op1=ALU.min,
             )
 
         def floor_at(s, t):
-            nc.vector.scalar_tensor_tensor(
-                out=held[s][:, t, :], in0=near[s][t][:], scalar=band[:, t : t + 1], in1=capped[s][t][:],
-                op0=ALU.subtract, op1=ALU.max,
-            )
+            nc.vector.tensor_tensor(out=held[s][:, t, :], in0=near[s][t][:], in1=capped[s][t][:], op=ALU.max)
 
         def weigh(t):
             nc.vector.tensor_tensor(out=y[0][:, t, :], in0=held[0][:, t, :], in1=rw_rows[:, :J_MAIN], op=ALU.mult)

@@ -22,7 +22,7 @@ K_PASS = P * PACK
 BANK = 512
 LIST_GROUP = 16
 J_MAIN = 384
-CAST_VECTOR_EIGHTHS = 5
+CAST_CUT = 84
 
 
 def tile_moe_expert_held_near_shared_pl_kernel(
@@ -55,17 +55,17 @@ def tile_moe_expert_held_near_shared_pl_kernel(
         nc.gpsimd.iota(column_less_row[:], pattern=[[1, P]], base=0, channel_multiplier=-1)
         nc.vector.tensor_scalar(out=identity[:], in0=column_less_row[:], scalar1=0.0, scalar2=None, op0=ALU.is_equal)
 
-        ws_pieces = [(0, 0, N // 2), (0, N // 2, N), (1, 0, N // 2), (1, N // 2, N)]
-        ws_raw = [sb.tile([P, PACK, c1 - c0], F32, name=f"ws_raw{i}", tag=f"ws_raw{i}", align_bytes=64) for i, (g, c0, c1) in enumerate(ws_pieces)]
+        ws_pieces = [(g, j0) for g in range(passes) for j0 in (0, 2)]
+        ws_raw = [sb.tile([P, 2, N], F32, name=f"ws_raw{i}") for i in range(len(ws_pieces))]
         xt_codes = [sb.tile([P, 2 * T], U8, name=f"xt_codes{g}", align_bytes=64) for g in range(passes)]
 
         def load_ws(i):
-            g, c0, c1 = ws_pieces[i]
-            rows = ws[g * K_PASS : (g + 1) * K_PASS, c0:c1]
-            nc.sync.dma_start(out=ws_raw[i][:], in_=rows.rearrange("(p j) n -> p j n", j=PACK))
+            g, j0 = ws_pieces[i]
+            rows = ws[g * K_PASS : (g + 1) * K_PASS, :].rearrange("(p j) n -> p j n", j=PACK)
+            nc.sync.dma_start(out=ws_raw[i][:], in_=rows[:, j0 : j0 + 2, :])
 
         nc.gpsimd.dma_start(out=rw_cols[:], in_=rw.rearrange("o (p c) -> (o p) c", c=PACK))
-        load_scale_rows(nc.gpsimd, we_plane_raw, we_scales)
+        load_scale_rows(nc.gpsimd, xe_plane, xe_scales)
         load_ws(0)
         load_ws(1)
         load_scale_rows(nc.sync, xt_plane, xt_scales)
@@ -76,11 +76,11 @@ def tile_moe_expert_held_near_shared_pl_kernel(
         load_ws(3)
         nc.sync.dma_start(out=xt_codes[1][:].bitcast(I32), in_=xt_words[1].bitcast(I32))
         nc.sync.dma_start(out=band[:], in_=bd.rearrange("(p t) o -> p (t o)", t=PACK))
-        offsets = sb.tile([P, J // LIST_GROUP], U16)
-        nc.sync.dma_start(offsets[:], offs)
+        load_scale_rows(nc.sync, we_plane_raw, we_scales)
         xe_codes = sb.tile([P, PACK * J], U8, align_bytes=64)
         nc.sync.dma_start(out=xe_codes[:].bitcast(I32), in_=xe_words[0].rearrange("p c r -> p (c r)").bitcast(I32))
-        load_scale_rows(nc.sync, xe_plane, xe_scales)
+        offsets = sb.tile([P, J // LIST_GROUP], U16)
+        nc.sync.dma_start(offsets[:], offs)
 
         rw_bank = psum.tile([P, PACK, P], F32, tag="p3")
         for c in range(PACK):
@@ -88,23 +88,16 @@ def tile_moe_expert_held_near_shared_pl_kernel(
         rw_rows = sb.tile([P, J], F32)
         nc.scalar.copy(out=rw_rows[:].rearrange("x (p c) -> x p c", c=PACK), in_=rw_bank[:].rearrange("x c p -> x p c"))
 
-        minus_band = sb.tile([P, PACK], F32)
-        twice_band = sb.tile([P, PACK], F32)
-        nc.vector.tensor_scalar(out=minus_band[:], in0=band[:], scalar1=-1.0, scalar2=None, op0=ALU.mult)
-        nc.vector.tensor_scalar(out=twice_band[:], in0=band[:], scalar1=2.0, scalar2=None, op0=ALU.mult)
-
-        ws_bf = [sb.tile([P, PACK * N], BF16, name=f"ws_bf{g}", align_bytes=64) for g in range(passes)]
+        ws_bf = [sb.tile([P, PACK * N], BF16, name=f"ws_bf{g}", tag=f"ws_bf{g}", align_bytes=64) for g in range(passes)]
         ws_codes = [sb.tile([P, N], U32, name=f"ws_codes{g}", align_bytes=64) for g in range(passes)]
         ws_plane = [sb.tile([P, N], U8, name=f"ws_plane{g}", align_bytes=64) for g in range(passes)]
 
         def round_ws(i):
-            g, c0, c1 = ws_pieces[i]
-            m0, count = c0 // PACK, (c1 - c0) // PACK
-            cut = count * CAST_VECTOR_EIGHTHS // 8
+            g, j0 = ws_pieces[i]
             src = ws_raw[i][:].rearrange("p j (m t) -> p m j t", t=PACK)
-            dst = ws_bf[g][:].rearrange("p (t m j) -> p m j t", t=PACK, j=PACK)
-            nc.vector.tensor_copy(out=dst[:, m0 : m0 + cut], in_=src[:, :cut])
-            nc.scalar.copy(out=dst[:, m0 + cut : m0 + count], in_=src[:, cut:])
+            dst = ws_bf[g][:].rearrange("p (t m j) -> p m j t", t=PACK, j=PACK)[:, :, j0 : j0 + 2, :]
+            nc.vector.tensor_copy(out=dst[:, :CAST_CUT], in_=src[:, :CAST_CUT])
+            nc.scalar.copy(out=dst[:, CAST_CUT:], in_=src[:, CAST_CUT:])
 
         def quantise_ws(g, t0, t1):
             nc.vector.quantize_mx(
@@ -119,6 +112,11 @@ def tile_moe_expert_held_near_shared_pl_kernel(
             quantise_ws(g, 0, 1)
             quantise_ws(g, 1, 2)
             quantise_ws(g, 2, 4)
+
+        minus_band = sb.tile([P, PACK], F32)
+        twice_band = sb.tile([P, PACK], F32)
+        nc.vector.tensor_scalar(out=minus_band[:], in0=band[:], scalar1=-1.0, scalar2=None, op0=ALU.mult)
+        nc.vector.tensor_scalar(out=twice_band[:], in0=band[:], scalar1=2.0, scalar2=None, op0=ALU.mult)
 
         u_banks = {}
 
@@ -152,7 +150,7 @@ def tile_moe_expert_held_near_shared_pl_kernel(
                     shared_pass(t, h, g)
 
         we_codes = sb.tile([P, 2 * N], U8, align_bytes=64)
-        we_plane = sb.tile([P, N], U8, tag="ws_raw1", align_bytes=64)
+        we_plane = sb.tile([P, N], U8, tag="ws_bf1", align_bytes=64)
         nc.vector.tensor_copy(
             out=we_codes[:].bitcast(U16).rearrange("p (t m) -> p t m", t=PACK),
             in_=we_raw[:].bitcast(U16).rearrange("p (m t) -> p t m", t=PACK),
@@ -191,27 +189,29 @@ def tile_moe_expert_held_near_shared_pl_kernel(
         y_bf = sb.tile([P, J, PACK], BF16, align_bytes=64)
 
         stretches = [(0, J_MAIN), (J_MAIN, J)]
-        near = [[sb.tile([P, j1 - j0], F32, name=f"near{s}{t}") for t in range(PACK)] for s, (j0, j1) in enumerate(stretches)]
-        capped = [[sb.tile([P, j1 - j0], F32, name=f"capped{s}{t}") for t in range(PACK)] for s, (j0, j1) in enumerate(stretches)]
+        near = [{}, {}]
+        capped = [sb.tile([P, PACK, j1 - j0], F32, name=f"capped{s}") for s, (j0, j1) in enumerate(stretches)]
         held = [sb.tile([P, PACK, j1 - j0], F32, name=f"held{s}") for s, (j0, j1) in enumerate(stretches)]
         y = [sb.tile([P, PACK, j1 - j0], F32, name=f"y{s}") for s, (j0, j1) in enumerate(stretches)]
 
         def look_up(s, t):
             j0, j1 = stretches[s]
-            nc.vector.tensor_copy(near[s][t][:], u_rows[t][:].indirect(offsets[:, j0 // LIST_GROUP : j1 // LIST_GROUP]))
+            if s == 0:
+                near[s][t] = sb.tile([P, J_MAIN], F32, name=f"near_main{t}", tag=f"near{t % 2}")[:]
+            nc.vector.tensor_copy(near[s][t], u_rows[t][:].indirect(offsets[:, j0 // LIST_GROUP : j1 // LIST_GROUP]))
 
         def cap(s, t):
             j0, j1 = stretches[s]
             nc.vector.scalar_tensor_tensor(
-                out=capped[s][t][:], in0=near[s][t][:], scalar=twice_band[:, t : t + 1], in1=p_banks[t][:, j0:j1],
+                out=capped[s][:, t, :], in0=near[s][t], scalar=twice_band[:, t : t + 1], in1=p_banks[t][:, j0:j1],
                 op0=ALU.add, op1=ALU.min,
             )
 
         def floor_at(s, t):
-            nc.vector.tensor_tensor(out=held[s][:, t, :], in0=near[s][t][:], in1=capped[s][t][:], op=ALU.max)
+            nc.vector.tensor_tensor(out=held[s][:, t, :], in0=near[s][t], in1=capped[s][:, t, :], op=ALU.max)
 
         def weigh(t):
-            nc.vector.tensor_tensor(out=y[0][:, t, :], in0=held[0][:, t, :], in1=rw_rows[:, :J_MAIN], op=ALU.mult)
+            nc.gpsimd.tensor_tensor(out=y[0][:, t, :], in0=held[0][:, t, :], in1=rw_rows[:, :J_MAIN], op=ALU.mult)
             nc.sync.dma_start(out=out_rows[:, t, :J_MAIN], in_=y[0][:, t, :])
 
         def round_y(copy, s, j0, j1):
@@ -235,6 +235,9 @@ def tile_moe_expert_held_near_shared_pl_kernel(
             floor_at(0, t - 1)
             cap(0, t)
             weigh(t - 1)
+        near_last = sb.tile([P, PACK, J - J_MAIN], F32, tag="near0")
+        for t in range(PACK):
+            near[1][t] = near_last[:, t, :]
         look_up(1, 0)
         floor_at(0, PACK - 1)
         look_up(1, 1)
@@ -245,17 +248,16 @@ def tile_moe_expert_held_near_shared_pl_kernel(
         look_up(1, 3)
         for t in range(PACK):
             cap(1, t)
-        for t in range(PACK):
-            floor_at(1, t)
-        quantise_y(0, 256)
+        nc.vector.tensor_tensor(out=held[1][:], in0=near_last[:], in1=capped[1][:], op=ALU.max)
         nc.vector.tensor_tensor(
             out=y[1][:], in0=held[1][:],
             in1=rw_rows[:, J_MAIN:].unsqueeze(1).to_broadcast([P, PACK, J - J_MAIN]), op=ALU.mult,
         )
-        nc.sync.dma_start(out=out_rows[:, :, J_MAIN:], in_=y[1][:])
+        nc.scalar.dma_start(out=out_rows[:, :, J_MAIN:], in_=y[1][:])
+        quantise_y(0, 256)
+        round_y(nc.vector.tensor_copy, 1, J_MAIN, J)
         quantise_y(256, J_MAIN)
         nc.sync.dma_start(out=out_words[:, :J_MAIN], in_=y_codes[:, :J_MAIN].bitcast(I32))
-        round_y(nc.vector.tensor_copy, 1, J_MAIN, J)
         quantise_y(J_MAIN, J)
         nc.sync.dma_start(out=out_words[:, J_MAIN:], in_=y_codes[:, J_MAIN:].bitcast(I32))
         for q in range(4):

@@ -221,6 +221,9 @@ def tile_moe_expert_held_near_shared_pl_kernel(
                 in_=y[s][:, :, j0 - base : j1 - base].rearrange("p t (c i) -> p c t i", i=4),
             )
 
+        def round_pair(ts, j0, j1):
+            nc.scalar.copy(out=y_bf[:, j0:j1, ts], in_=y[0][:, ts, j0:j1].rearrange("p t j -> p j t"))
+
         def quantise_y(j0, j1):
             nc.vector.quantize_mx(
                 out=y_codes[:, j0:j1].bitcast(FP8X4),
@@ -235,25 +238,26 @@ def tile_moe_expert_held_near_shared_pl_kernel(
             floor_at(0, t - 1)
             cap(0, t)
             weigh(t - 1)
-        near_last = sb.tile([P, PACK, J - J_MAIN], F32, tag="near0")
+        floor_at(0, PACK - 1)
+        weigh(PACK - 1)
+        round_pair(slice(0, 2), 0, J_MAIN)
+        round_pair(slice(2, PACK), 0, 256)
+        round_pair(slice(2, PACK), 256, J_MAIN)
+        near_last = sb.tile([P, PACK, J - J_MAIN], F32, tag="near1")
         for t in range(PACK):
             near[1][t] = near_last[:, t, :]
-        look_up(1, 0)
-        floor_at(0, PACK - 1)
-        look_up(1, 1)
-        weigh(PACK - 1)
-        round_y(nc.scalar.copy, 0, 0, 256)
-        round_y(nc.scalar.copy, 0, 256, J_MAIN)
-        look_up(1, 2)
-        look_up(1, 3)
+            look_up(1, t)
         for t in range(PACK):
             cap(1, t)
-        nc.vector.tensor_tensor(out=held[1][:], in0=near_last[:], in1=capped[1][:], op=ALU.max)
-        nc.vector.tensor_tensor(
-            out=y[1][:], in0=held[1][:],
-            in1=rw_rows[:, J_MAIN:].unsqueeze(1).to_broadcast([P, PACK, J - J_MAIN]), op=ALU.mult,
-        )
-        nc.scalar.dma_start(out=out_rows[:, :, J_MAIN:], in_=y[1][:])
+        pairs = [slice(0, 2), slice(2, PACK)]
+        for ts in pairs:
+            nc.vector.tensor_tensor(out=held[1][:, ts, :], in0=near_last[:, ts, :], in1=capped[1][:, ts, :], op=ALU.max)
+        for ts in pairs:
+            nc.vector.tensor_tensor(
+                out=y[1][:, ts, :], in0=held[1][:, ts, :],
+                in1=rw_rows[:, J_MAIN:].unsqueeze(1).to_broadcast([P, 2, J - J_MAIN]), op=ALU.mult,
+            )
+            nc.sync.dma_start(out=out_rows[:, ts, J_MAIN:], in_=y[1][:, ts, :])
         quantise_y(0, 256)
         round_y(nc.vector.tensor_copy, 1, J_MAIN, J)
         quantise_y(256, J_MAIN)

from contextlib import ExitStack

import concourse.mybir as mybir

K, L, T, J, N = 1024, 512, 1024, 512, 512
FLOPS = 2 * K * N * T + 2 * L * N * J

F32 = mybir.dt.float32
BF16 = mybir.dt.bfloat16
I32 = mybir.dt.int32
U32 = mybir.dt.uint32
U16 = mybir.dt.uint16
U8 = mybir.dt.uint8
FP8X4 = mybir.dt.float8_e4m3fn_x4
FP4X4 = mybir.dt.float4_e2m1fn_x4
ALU = mybir.AluOpType
ACT = mybir.ActivationFunctionType

P = 128
PACK = 4
K_PASS = P * PACK
BANK = 512
LIST_GROUP = 16
J_MAIN = 384
CAST_CUT = 84


def tile_moe_expert_held_near_shared_pl_kernel(
    tc, xt_words, xt_scales, ws, xe_words, xe_scales, we_words, we_scales, bd, rw, offs, out_0, out_1, out_2
):
    nc = tc.nc
    passes = K // K_PASS
    halves = T // BANK

    with ExitStack() as ctx:
        sb = ctx.enter_context(tc.tile_pool(name="sb", bufs=1))
        psum = ctx.enter_context(tc.psum_pool(name="psum", bufs=1))

        def load_scale_rows(queue, plane, rows):
            for q in range(4):
                queue.dma_start(
                    out=plane[32 * q : 32 * q + 4].bitcast(I32),
                    in_=rows[:, 4 * q : 4 * q + 4, :].rearrange("z r c -> r z c").bitcast(I32),
                )

        xt_plane = sb.tile([P, passes, T], U8, align_bytes=64)
        xe_plane = sb.tile([P, 1, J], U8, align_bytes=64)
        we_plane_raw = sb.tile([P, 1, N], U8, align_bytes=64)
        nc.vector.memset(we_plane_raw[:].bitcast(I32), 0)

        band = sb.tile([P, PACK], F32)
        rw_cols = sb.tile([P, PACK], F32)
        identity = sb.tile([P, P], F32)
        column_less_row = sb.tile([P, P], I32)
        nc.gpsimd.iota(column_less_row[:], pattern=[[1, P]], base=0, channel_multiplier=-1)
        nc.vector.tensor_scalar(out=identity[:], in0=column_less_row[:], scalar1=0.0, scalar2=None, op0=ALU.is_equal)

        ws_pieces = [(g, j0) for g in range(passes) for j0 in (0, 2)]
        ws_raw = [sb.tile([P, 2, N], F32, name=f"ws_raw{i}") for i in range(len(ws_pieces))]
        xt_codes = [sb.tile([P, 2 * T], U8, name=f"xt_codes{g}", align_bytes=64) for g in range(passes)]

        def load_ws(i):
            g, j0 = ws_pieces[i]
            rows = ws[g * K_PASS : (g + 1) * K_PASS, :].rearrange("(p j) n -> p j n", j=PACK)
            nc.sync.dma_start(out=ws_raw[i][:], in_=rows[:, j0 : j0 + 2, :])

        nc.gpsimd.dma_start(out=rw_cols[:], in_=rw.rearrange("o (p c) -> (o p) c", c=PACK))
        load_scale_rows(nc.gpsimd, xe_plane, xe_scales)
        load_ws(0)
        load_ws(1)
        load_scale_rows(nc.sync, xt_plane, xt_scales)
        nc.sync.dma_start(out=xt_codes[0][:].bitcast(I32), in_=xt_words[0].bitcast(I32))
        we_raw = sb.tile([P, 2 * N], U8, align_bytes=64)
        nc.sync.dma_start(out=we_raw[:].bitcast(I32), in_=we_words[0].bitcast(I32))
        load_ws(2)
        load_ws(3)
        nc.sync.dma_start(out=xt_codes[1][:].bitcast(I32), in_=xt_words[1].bitcast(I32))
        nc.sync.dma_start(out=band[:], in_=bd.rearrange("(p t) o -> p (t o)", t=PACK))
        load_scale_rows(nc.sync, we_plane_raw, we_scales)
        xe_codes = sb.tile([P, PACK * J], U8, align_bytes=64)
        nc.sync.dma_start(out=xe_codes[:].bitcast(I32), in_=xe_words[0].rearrange("p c r -> p (c r)").bitcast(I32))
        offsets = sb.tile([P, J // LIST_GROUP], U16)
        nc.sync.dma_start(offsets[:], offs)

        rw_bank = psum.tile([P, PACK, P], F32, tag="p3")
        for c in range(PACK):
            nc.tensor.transpose(rw_bank[:, c, :], rw_cols[:, c : c + 1].to_broadcast([P, P]), identity[:])
        rw_rows = sb.tile([P, J], F32)
        nc.scalar.copy(out=rw_rows[:].rearrange("x (p c) -> x p c", c=PACK), in_=rw_bank[:].rearrange("x c p -> x p c"))

        ws_bf = [sb.tile([P, PACK * N], BF16, name=f"ws_bf{g}", tag=f"ws_bf{g}", align_bytes=64) for g in range(passes)]
        ws_codes = [sb.tile([P, N], U32, name=f"ws_codes{g}", align_bytes=64) for g in range(passes)]
        ws_plane = [sb.tile([P, N], U8, name=f"ws_plane{g}", align_bytes=64) for g in range(passes)]

        def round_ws(i):
            g, j0 = ws_pieces[i]
            src = ws_raw[i][:].rearrange("p j (m t) -> p m j t", t=PACK)
            dst = ws_bf[g][:].rearrange("p (t m j) -> p m j t", t=PACK, j=PACK)[:, :, j0 : j0 + 2, :]
            nc.vector.tensor_copy(out=dst[:, :CAST_CUT], in_=src[:, :CAST_CUT])
            nc.scalar.copy(out=dst[:, CAST_CUT:], in_=src[:, CAST_CUT:])

        def quantise_ws(g, t0, t1):
            nc.vector.quantize_mx(
                out=ws_codes[g][:, t0 * P : t1 * P].bitcast(FP8X4),
                scales=ws_plane[g][:, t0 * P : t1 * P],
                in_=ws_bf[g][:, t0 * K_PASS : t1 * K_PASS],
            )

        for g in range(passes):
            round_ws(2 * g)
            round_ws(2 * g + 1)
            quantise_ws(g, 0, 1)
            quantise_ws(g, 1, 2)
            quantise_ws(g, 2, 4)

        minus_band = sb.tile([P, PACK], F32)
        twice_band = sb.tile([P, PACK], F32)
        nc.vector.tensor_scalar(out=minus_band[:], in0=band[:], scalar1=-1.0, scalar2=None, op0=ALU.mult)
        nc.vector.tensor_scalar(out=twice_band[:], in0=band[:], scalar1=2.0, scalar2=None, op0=ALU.mult)

        u_banks = {}

        def shared_pass(t, h, g):
            if g == 0:
                u_banks[t, h] = psum.tile([P, BANK], F32, name=f"u_bank{t}{h}", tag=f"u{(halves * t + h) % 4}")
            nc.tensor.matmul_mx(
                out=u_banks[t, h][:],
                lhsT=ws_codes[g][:, t * P : (t + 1) * P].bitcast(FP8X4),
                lhsT_scale=ws_plane[g][:, t * P : (t + 1) * P],
                rhs=xt_codes[g][:, 2 * h * BANK : 2 * (h + 1) * BANK].bitcast(FP4X4),
                rhs_scale=xt_plane[:, g, h * BANK : (h + 1) * BANK],
                start=(g == 0),
                stop=(g == passes - 1),
            )

        u_rows = [sb.tile([P, T], F32, name=f"u_rows{t}") for t in range(PACK)]

        def empty_u(t, h):
            dst = u_rows[t][:, h * BANK : (h + 1) * BANK]
            if (t, h) == (0, 1):
                nc.vector.tensor_scalar(
                    out=dst, in0=u_banks[t, h][:], scalar1=minus_band[:, t : t + 1], scalar2=None, op0=ALU.add
                )
            else:
                nc.scalar.activation(out=dst, in_=u_banks[t, h][:], func=ACT.Identity, bias=minus_band[:, t : t + 1])

        for g in range(passes):
            for t in range(2):
                for h in range(halves):
                    shared_pass(t, h, g)

        we_codes = sb.tile([P, 2 * N], U8, align_bytes=64)
        we_plane = sb.tile([P, N], U8, tag="ws_bf1", align_bytes=64)
        nc.vector.tensor_copy(
            out=we_codes[:].bitcast(U16).rearrange("p (t m) -> p t m", t=PACK),
            in_=we_raw[:].bitcast(U16).rearrange("p (m t) -> p t m", t=PACK),
        )
        nc.vector.tensor_copy(
            out=we_plane[:].rearrange("p (t m) -> p t m", t=PACK),
            in_=we_plane_raw[:, 0, :].rearrange("p (m t) -> p t m", t=PACK),
        )
        for t in range(2):
            for h in range(halves):
                empty_u(t, h)

        p_banks = []
        for t in range(PACK):
            p_bank = psum.tile([P, J], F32, name=f"p_bank{t}", tag=f"p{t}")
            nc.tensor.matmul_mx(
                out=p_bank[:],
                lhsT=we_codes[:, 2 * t * P : 2 * (t + 1) * P].bitcast(FP4X4),
                lhsT_scale=we_plane[:, t * P : (t + 1) * P],
                rhs=xe_codes[:].bitcast(FP8X4),
                rhs_scale=xe_plane[:, 0, :],
                start=True,
                stop=True,
            )
            p_banks.append(p_bank)
        for t in range(2, PACK):
            for h in range(halves):
                for g in range(passes):
                    shared_pass(t, h, g)
                empty_u(t, h)

        out_rows = out_0.rearrange("(p t) j -> p t j", t=PACK)
        out_words = out_1[0].rearrange("p c r -> p (c r)").bitcast(I32)
        y_codes = sb.tile([P, J], U32, align_bytes=64)
        y_plane = sb.tile([P, J], U8, align_bytes=64)
        y_bf = sb.tile([P, J, PACK], BF16, align_bytes=64)

        stretches = [(0, J_MAIN), (J_MAIN, J)]
        near = [{}, {}]
        capped = [sb.tile([P, PACK, j1 - j0], F32, name=f"capped{s}") for s, (j0, j1) in enumerate(stretches)]
        held = [sb.tile([P, PACK, j1 - j0], F32, name=f"held{s}") for s, (j0, j1) in enumerate(stretches)]
        y = [sb.tile([P, PACK, j1 - j0], F32, name=f"y{s}") for s, (j0, j1) in enumerate(stretches)]

        def look_up(s, t):
            j0, j1 = stretches[s]
            if s == 0:
                near[s][t] = sb.tile([P, J_MAIN], F32, name=f"near_main{t}", tag=f"near{t % 2}")[:]
            nc.vector.tensor_copy(near[s][t], u_rows[t][:].indirect(offsets[:, j0 // LIST_GROUP : j1 // LIST_GROUP]))

        def cap(s, t):
            j0, j1 = stretches[s]
            nc.vector.scalar_tensor_tensor(
                out=capped[s][:, t, :], in0=near[s][t], scalar=twice_band[:, t : t + 1], in1=p_banks[t][:, j0:j1],
                op0=ALU.add, op1=ALU.min,
            )

        def floor_at(s, t):
            nc.vector.tensor_tensor(out=held[s][:, t, :], in0=near[s][t], in1=capped[s][:, t, :], op=ALU.max)

        def weigh(t):
            nc.gpsimd.tensor_tensor(out=y[0][:, t, :], in0=held[0][:, t, :], in1=rw_rows[:, :J_MAIN], op=ALU.mult)
            nc.sync.dma_start(out=out_rows[:, t, :J_MAIN], in_=y[0][:, t, :])

        def round_y(copy, s, j0, j1):
            base = stretches[s][0]
            copy(
                out=y_bf[:, j0:j1, :].rearrange("p (c i) t -> p c t i", i=4),
                in_=y[s][:, :, j0 - base : j1 - base].rearrange("p t (c i) -> p c t i", i=4),
            )

        def round_pair(ts, j0, j1):
            nc.scalar.copy(out=y_bf[:, j0:j1, ts], in_=y[0][:, ts, j0:j1].rearrange("p t j -> p j t"))

        def quantise_y(j0, j1):
            nc.vector.quantize_mx(
                out=y_codes[:, j0:j1].bitcast(FP8X4),
                scales=y_plane[:, j0:j1],
                in_=y_bf[:, j0:j1, :].rearrange("p j t -> p (j t)"),
            )

        look_up(0, 0)
        cap(0, 0)
        for t in range(1, PACK):
            look_up(0, t)
            floor_at(0, t - 1)
            cap(0, t)
            weigh(t - 1)
        floor_at(0, PACK - 1)
        weigh(PACK - 1)
        round_pair(slice(0, 2), 0, J_MAIN)
        round_pair(slice(2, PACK), 0, 256)
        round_pair(slice(2, PACK), 256, J_MAIN)
        near_last = sb.tile([P, PACK, J - J_MAIN], F32, tag="near1")
        for t in range(PACK):
            near[1][t] = near_last[:, t, :]
            look_up(1, t)
        for t in range(PACK):
            cap(1, t)
        pairs = [slice(0, 2), slice(2, PACK)]
        for ts in pairs:
            nc.vector.tensor_tensor(out=held[1][:, ts, :], in0=near_last[:, ts, :], in1=capped[1][:, ts, :], op=ALU.max)
        for ts in pairs:
            nc.vector.tensor_tensor(
                out=y[1][:, ts, :], in0=held[1][:, ts, :],
                in1=rw_rows[:, J_MAIN:].unsqueeze(1).to_broadcast([P, 2, J - J_MAIN]), op=ALU.mult,
            )
            nc.sync.dma_start(out=out_rows[:, ts, J_MAIN:], in_=y[1][:, ts, :])
        quantise_y(0, 256)
        round_y(nc.vector.tensor_copy, 1, J_MAIN, J)
        quantise_y(256, J_MAIN)
        nc.sync.dma_start(out=out_words[:, :J_MAIN], in_=y_codes[:, :J_MAIN].bitcast(I32))
        quantise_y(J_MAIN, J)
        nc.sync.dma_start(out=out_words[:, J_MAIN:], in_=y_codes[:, J_MAIN:].bitcast(I32))
        for q in range(4):
            queue = nc.scalar if q % 2 == 0 else nc.sync
            queue.dma_start(
                out=out_2[0, 4 * q : 4 * q + 4, :].bitcast(I32),
                in_=y_plane[32 * q : 32 * q + 4, :].bitcast(I32),
            )
